import numpy as np
import ml_dtypes


def mxq(x, axis, fmt="e4m3"):
    dtype, down = {"e4m3": (ml_dtypes.float8_e4m3fn, 7), "e5m2": (ml_dtypes.float8_e5m2, 14)}[fmt]
    v = np.moveaxis(np.asarray(x, np.float32).astype(ml_dtypes.bfloat16).astype(np.float64), axis, -1)
    blocks = v.reshape(v.shape[:-1] + (-1, 32))
    amax = np.abs(blocks).max(-1, keepdims=True)
    byte = np.maximum(np.where(amax > 0, np.frexp(amax)[1] - 1 + 127, 0) - down, 1)
    scale = np.exp2(byte - 127.0)
    codes = (blocks / scale).astype(np.float32).astype(dtype).astype(np.float64)
    return np.moveaxis((codes * scale).reshape(v.shape), -1, axis)


WIDE = False


def mx_kscale(k):
    if not WIDE:
        return np.ones(k)
    levels = np.array([10, -10, 5, -5, 0])
    if k % 512:
        return np.exp2(np.random.permutation(np.resize(levels, k // 32))).repeat(32)
    a = np.empty((k // 512, 16))
    for p in range(k // 512):
        a[p, :8] = np.random.permutation(np.resize(levels, 8))
        for g in range(8):
            far = levels[np.abs(levels - a[p, g]) >= 10]
            a[p, g + 8] = far[np.random.randint(len(far))]
    return np.exp2(a.ravel()).repeat(32)


def f64(x):
    return np.asarray(x).astype(np.float64)


def striped(idx):
    return np.tile(np.asarray(idx).reshape(-1, 16).T, (8, 1)).astype(np.uint16)


def unstriped(offs):
    return offs[:16].T.reshape(-1).astype(np.int64)


B, N, T, D, DV, NQ = 1, 512, 1024, 512, 0, 512
PAGE = 128


def setup_inputs():
    n = np.random.standard_normal
    pages = np.random.permutation(T // PAGE)[:B * N // PAGE]
    idx = (pages[:, None] * PAGE + np.arange(PAGE)[None, :]).reshape(-1)
    s = mx_kscale(D)[:, None]
    r = np.random.uniform(0.5, 2.0, T)
    return {
        "qT": (n((B, D, NQ)) * s * (1.00 / np.sqrt(D))).astype(np.float32),
        "kT": (n((D, T)) / s / r).astype(np.float32),
        "ts": np.tile(r, (128, 1)).astype(np.float32),
        "offs": striped(idx),
    }


def reference(qT, kT, ts, offs):
    idx = unstriped(offs)
    pick = lambda x: x[:, idx].reshape(x.shape[0], B, N).transpose(1, 0, 2)
    a = mxq(f64(qT), 1, "e4m3").transpose(0, 2, 1) @ mxq(pick(f64(kT)), 1, "e4m3")
    a = a * pick(f64(ts))[:, :1, :]
    out = np.zeros((B, NQ, T))
    for b in range(B):
        out[b][:, idx[b * N:(b + 1) * N]] = a[b]
    return out

@@ -1,0 +1,132 @@
+from contextlib import ExitStack
+
+import concourse.mybir as mybir
+
+D_FEAT, NQ, T, N = 512, 512, 1024, 512
+P = 128
+PACK = 4
+FLOPS = 2 * D_FEAT * NQ * N
+
+F32 = mybir.dt.float32
+BF16 = mybir.dt.bfloat16
+U32 = mybir.dt.uint32
+U16 = mybir.dt.uint16
+U8 = mybir.dt.uint8
+FP8X4 = mybir.dt.float8_e4m3fn_x4
+MULT = mybir.AluOpType.mult
+
+
+def tile_attend_sddmm_ts_kernel(tc, qT, kT, ts, offs, out):
+    nc = tc.nc
+    k_rows = kT.rearrange("(p t) w -> p t w", t=PACK)
+    q_rows = qT.rearrange("b (p t) q -> p (b t) q", t=PACK)
+    out_rows = out.rearrange("b (m p) w -> p (b m) w", p=P)
+    half = N // 2
+
+    with ExitStack() as ctx:
+        keep = ctx.enter_context(tc.tile_pool(name="keep", bufs=1))
+        psum = ctx.enter_context(tc.psum_pool(name="psum", bufs=1))
+
+        offsets = keep.tile([P, N // 16], U16, name="offsets")
+        nc.sync.dma_start(offsets[:], offs)
+
+        k_pool = []
+        for t in range(PACK):
+            plane = keep.tile([P, T], F32, name="k_plane%d" % t)
+            nc.sync.dma_start(plane[:], k_rows[:, t, :])
+            k_pool.append(plane)
+
+        q_raw = []
+        ts_pool = keep.tile([P, T], F32, name="ts_pool")
+        for c0, w in ((0, 2 * P), (2 * P, P), (3 * P, P)):
+            raw = keep.tile([P, PACK, w], F32, name="q_raw%d" % c0)
+            nc.sync.dma_start(raw[:], q_rows[:, :, c0 : c0 + w])
+            q_raw.extend(raw[:, :, c : c + P] for c in range(0, w, P))
+            if c0 == 0:
+                nc.sync.dma_start(ts_pool[:], ts)
+
+        windows = []
+        for m in range(NQ // P):
+            window = keep.tile([P, T], F32, name="window%d" % m)
+            nc.gpsimd.memset(window[:], 0.0)
+            windows.append(window)
+
+        q_codes, q_scales, q_grouped = {}, {}, {}
+
+        def group_queries(m):
+            grouped = keep.tile([P, P, PACK], BF16, name="q_grouped%d" % m, align_bytes=64)
+            nc.scalar.copy(grouped[:], q_raw[m].rearrange("p t c -> p c t"))
+            q_grouped[m] = grouped
+
+        def quantize_queries(m):
+            codes = keep.tile([P, P], U32, name="q_codes%d" % m, align_bytes=64)
+            scales = keep.tile([P, P], U8, name="q_scales%d" % m, align_bytes=64)
+            nc.vector.quantize_mx(out=codes[:].bitcast(FP8X4), scales=scales[:], in_=q_grouped[m][:].rearrange("p c t -> p (c t)"))
+            q_codes[m], q_scales[m] = codes, scales
+
+        scores = {}
+
+        def score(m, pieces):
+            tag = "q_raw%d" % ((m + 1) * P) if m in (1, 2) else "scores%d" % m
+            scores[m] = keep.tile([P, N], F32, name="scores%d" % m, tag=tag)
+            width = N // pieces
+            for h in range(pieces):
+                cols = slice(h * width, (h + 1) * width)
+                if pieces == 2:
+                    quantize_keys(cols)
+                acc = psum.tile([P, width], F32, name="acc%d_%d" % (m, h))
+                nc.tensor.matmul_mx(
+                    out=acc[:],
+                    lhsT=q_codes[m][:].bitcast(FP8X4),
+                    lhsT_scale=q_scales[m][:],
+                    rhs=k_codes[:, cols].bitcast(FP8X4),
+                    rhs_scale=k_scales[:, cols],
+                    start=True,
+                    stop=True,
+                )
+                nc.scalar.copy(scores[m][:, cols], acc[:])
+
+        def place(m):
+            nc.vector.tensor_tensor(windows[m][:].indirect(offsets[:]), scores[m][:], ts_listed[:], MULT)
+            nc.sync.dma_start(out_rows[:, m, :], windows[m][:])
+
+        g01 = keep.tile([P, 2, N], F32, name="g01")
+        g23 = keep.tile([P, 2, N], F32, name="g23")
+        k_grouped = keep.tile([P, N, PACK], BF16, name="k_grouped", align_bytes=64)
+        k_codes = keep.tile([P, N], U32, name="k_codes", align_bytes=64)
+        k_scales = keep.tile([P, N], U8, name="k_scales", align_bytes=64)
+
+        def quantize_keys(cols):
+            nc.vector.quantize_mx(
+                out=k_codes[:, cols].bitcast(FP8X4),
+                scales=k_scales[:, cols],
+                in_=k_grouped[:, cols, :].rearrange("p c t -> p (c t)"),
+            )
+
+        nc.vector.tensor_copy(g01[:, 0, :], k_pool[0][:].indirect(offsets[:]))
+        nc.vector.tensor_copy(g01[:, 1, :], k_pool[1][:].indirect(offsets[:]))
+        nc.scalar.copy(k_grouped[:, :, 0:2], g01[:].rearrange("p t c -> p c t"))
+        nc.vector.tensor_copy(g23[:, 0, :], k_pool[2][:].indirect(offsets[:]))
+        for h in range(2):
+            cols = slice(h * half, (h + 1) * half)
+            nc.vector.tensor_copy(g23[:, 1, cols], k_pool[3][:].indirect(offsets[:, h * (half // 16) : (h + 1) * (half // 16)]))
+        for copy, cols in ((nc.scalar.copy, slice(384, 512)), (nc.vector.tensor_copy, slice(0, 256)), (nc.vector.tensor_copy, slice(256, 384))):
+            copy(k_grouped[:, cols, 2:4], g23[:, :, cols].rearrange("p t c -> p c t"))
+        group_queries(0)
+        quantize_queries(0)
+        group_queries(1)
+        score(0, 2)
+        quantize_queries(1)
+        ts_listed = keep.tile([P, N], F32, name="ts_listed")
+        nc.vector.tensor_copy(ts_listed[:], ts_pool[:].indirect(offsets[:]))
+        group_queries(2)
+        place(0)
+        quantize_queries(2)
+        score(1, 1)
+        group_queries(3)
+        quantize_queries(3)
+        place(1)
+        score(2, 1)
+        place(2)
+        score(3, 1)
+        place(3)

@@ -1,6 +1,7 @@
 from contextlib import ExitStack
 
 import concourse.mybir as mybir
+from concourse.masks import make_identity
 
 D_FEAT, NQ, T, N = 512, 512, 1024, 512
 P = 128
@@ -22,6 +23,7 @@ def tile_attend_sddmm_ts_kernel(tc, qT, kT, ts, offs, out):
     q_rows = qT.rearrange("b (p t) q -> p (b t) q", t=PACK)
     out_rows = out.rearrange("b (m p) w -> p (b m) w", p=P)
     half = N // 2
+    per = T // P
 
     with ExitStack() as ctx:
         keep = ctx.enter_context(tc.tile_pool(name="keep", bufs=1))
@@ -29,6 +31,8 @@ def tile_attend_sddmm_ts_kernel(tc, qT, kT, ts, offs, out):
 
         offsets = keep.tile([P, N // 16], U16, name="offsets")
         nc.sync.dma_start(offsets[:], offs)
+        ts_cols = keep.tile([P, per], F32, name="ts_cols")
+        nc.scalar.dma_start(ts_cols[:], ts[0:1, :].rearrange("o (p j) -> (o p) j", j=per))
 
         k_pool = []
         for t in range(PACK):
@@ -37,25 +41,34 @@ def tile_attend_sddmm_ts_kernel(tc, qT, kT, ts, offs, out):
             k_pool.append(plane)
 
         q_raw = []
-        ts_pool = keep.tile([P, T], F32, name="ts_pool")
-        for c0, w in ((0, 2 * P), (2 * P, P), (3 * P, P)):
+        for c0, w in ((0, P), (P, P), (2 * P, 2 * P)):
             raw = keep.tile([P, PACK, w], F32, name="q_raw%d" % c0)
             nc.sync.dma_start(raw[:], q_rows[:, :, c0 : c0 + w])
             q_raw.extend(raw[:, :, c : c + P] for c in range(0, w, P))
-            if c0 == 0:
-                nc.sync.dma_start(ts_pool[:], ts)
+
+        ident = keep.tile([P, P], F32, name="ident")
+        make_identity(nc, ident[:])
 
         windows = []
         for m in range(NQ // P):
             window = keep.tile([P, T], F32, name="window%d" % m)
-            nc.gpsimd.memset(window[:], 0.0)
+            nc.vector.memset(window[:], 0.0)
             windows.append(window)
+
+        ts_pool = keep.tile([P, T], F32, name="ts_pool")
+        ts_by_j = ts_pool[:].rearrange("p (n j) -> p n j", j=per)
+        for g in range(per // 4):
+            spread = psum.tile([P, 4, P], F32, name="spread%d" % g)
+            for j in range(4):
+                col = 4 * g + j
+                nc.tensor.transpose(spread[:, j, :], ts_cols[:, col : col + 1].to_broadcast([P, P]), ident[:])
+            nc.scalar.copy(ts_by_j[:, :, 4 * g : 4 * g + 4], spread[:].rearrange("p j n -> p n j"))
 
         q_codes, q_scales, q_grouped = {}, {}, {}
 
-        def group_queries(m):
+        def group_queries(m, copy):
             grouped = keep.tile([P, P, PACK], BF16, name="q_grouped%d" % m, align_bytes=64)
-            nc.scalar.copy(grouped[:], q_raw[m].rearrange("p t c -> p c t"))
+            copy(grouped[:].rearrange("p (c i) t -> p c t i", i=4), q_raw[m].rearrange("p t (c i) -> p c t i", i=4))
             q_grouped[m] = grouped
 
         def quantize_queries(m):
@@ -66,28 +79,28 @@ def tile_attend_sddmm_ts_kernel(tc, qT, kT, ts, offs, out):
 
         scores = {}
 
-        def score(m, pieces):
-            tag = "q_raw%d" % ((m + 1) * P) if m in (1, 2) else "scores%d" % m
-            scores[m] = keep.tile([P, N], F32, name="scores%d" % m, tag=tag)
-            width = N // pieces
-            for h in range(pieces):
-                cols = slice(h * width, (h + 1) * width)
-                if pieces == 2:
-                    quantize_keys(cols)
-                acc = psum.tile([P, width], F32, name="acc%d_%d" % (m, h))
-                nc.tensor.matmul_mx(
-                    out=acc[:],
-                    lhsT=q_codes[m][:].bitcast(FP8X4),
-                    lhsT_scale=q_scales[m][:],
-                    rhs=k_codes[:, cols].bitcast(FP8X4),
-                    rhs_scale=k_scales[:, cols],
-                    start=True,
-                    stop=True,
-                )
-                nc.scalar.copy(scores[m][:, cols], acc[:])
+        def score(m, cols):
+            if m not in scores:
+                scores[m] = keep.tile([P, N], F32, name="scores%d" % m)
+            acc = psum.tile([P, cols.stop - cols.start], F32, name="acc%d_%d" % (m, cols.start))
+            nc.tensor.matmul_mx(
+                out=acc[:],
+                lhsT=q_codes[m][:].bitcast(FP8X4),
+                lhsT_scale=q_scales[m][:],
+                rhs=k_codes[:, cols].bitcast(FP8X4),
+                rhs_scale=k_scales[:, cols],
+                start=True,
+                stop=True,
+            )
+            nc.scalar.copy(scores[m][:, cols], acc[:])
 
-        def place(m):
-            nc.vector.tensor_tensor(windows[m][:].indirect(offsets[:]), scores[m][:], ts_listed[:], MULT)
+        def listed(tile, cols):
+            return tile[:].indirect(offsets[:, cols.start // 16 : cols.stop // 16])
+
+        def place(m, cols):
+            nc.vector.tensor_tensor(listed(windows[m], cols), scores[m][:, cols], ts_listed[:, cols], MULT)
+
+        def store(m):
             nc.sync.dma_start(out_rows[:, m, :], windows[m][:])
 
         g01 = keep.tile([P, 2, N], F32, name="g01")
@@ -95,6 +108,8 @@ def tile_attend_sddmm_ts_kernel(tc, qT, kT, ts, offs, out):
         k_grouped = keep.tile([P, N, PACK], BF16, name="k_grouped", align_bytes=64)
         k_codes = keep.tile([P, N], U32, name="k_codes", align_bytes=64)
         k_scales = keep.tile([P, N], U8, name="k_scales", align_bytes=64)
+        ts_listed = keep.tile([P, N], F32, name="ts_listed")
+        whole, first, second = slice(0, N), slice(0, half), slice(half, N)
 
         def quantize_keys(cols):
             nc.vector.quantize_mx(
@@ -103,30 +118,36 @@ def tile_attend_sddmm_ts_kernel(tc, qT, kT, ts, offs, out):
                 in_=k_grouped[:, cols, :].rearrange("p c t -> p (c t)"),
             )
 
-        nc.vector.tensor_copy(g01[:, 0, :], k_pool[0][:].indirect(offsets[:]))
-        nc.vector.tensor_copy(g01[:, 1, :], k_pool[1][:].indirect(offsets[:]))
+        nc.vector.tensor_copy(g01[:, 0, :], listed(k_pool[0], whole))
+        nc.vector.tensor_copy(ts_listed[:], listed(ts_pool, whole))
+        nc.vector.tensor_copy(g01[:, 1, :], listed(k_pool[1], whole))
         nc.scalar.copy(k_grouped[:, :, 0:2], g01[:].rearrange("p t c -> p c t"))
-        nc.vector.tensor_copy(g23[:, 0, :], k_pool[2][:].indirect(offsets[:]))
-        for h in range(2):
-            cols = slice(h * half, (h + 1) * half)
-            nc.vector.tensor_copy(g23[:, 1, cols], k_pool[3][:].indirect(offsets[:, h * (half // 16) : (h + 1) * (half // 16)]))
-        for copy, cols in ((nc.scalar.copy, slice(384, 512)), (nc.vector.tensor_copy, slice(0, 256)), (nc.vector.tensor_copy, slice(256, 384))):
+        nc.vector.tensor_copy(g23[:, 0, :], listed(k_pool[2], whole))
+        for cols in (first, second):
+            nc.vector.tensor_copy(g23[:, 1, cols], listed(k_pool[3], cols))
+        for copy, cols in ((nc.scalar.copy, slice(0, 128)), (nc.vector.tensor_copy, slice(128, 256)), (nc.vector.tensor_copy, slice(256, 512))):
             copy(k_grouped[:, cols, 2:4], g23[:, :, cols].rearrange("p t c -> p c t"))
-        group_queries(0)
+        group_queries(0, nc.scalar.copy)
+        group_queries(1, nc.scalar.copy)
+        quantize_keys(first)
         quantize_queries(0)
-        group_queries(1)
-        score(0, 2)
+        quantize_keys(second)
+        score(0, first)
+        score(0, second)
         quantize_queries(1)
-        ts_listed = keep.tile([P, N], F32, name="ts_listed")
-        nc.vector.tensor_copy(ts_listed[:], ts_pool[:].indirect(offsets[:]))
-        group_queries(2)
-        place(0)
+        group_queries(2, nc.vector.tensor_copy)
+        place(0, first)
+        place(0, second)
+        store(0)
+        score(1, whole)
         quantize_queries(2)
-        score(1, 1)
-        group_queries(3)
+        group_queries(3, nc.scalar.copy)
+        place(1, whole)
+        store(1)
+        score(2, whole)
         quantize_queries(3)
-        place(1)
-        score(2, 1)
-        place(2)
-        score(3, 1)
-        place(3)
+        place(2, whole)
+        store(2)
+        score(3, whole)
+        place(3, whole)
+        store(3)

@@ -41,7 +41,7 @@ def tile_attend_sddmm_ts_kernel(tc, qT, kT, ts, offs, out):
             k_pool.append(plane)
 
         q_raw = []
-        for c0, w in ((0, P), (P, P), (2 * P, 2 * P)):
+        for c0, w in ((0, 2 * P), (2 * P, P), (3 * P, P)):
             raw = keep.tile([P, PACK, w], F32, name="q_raw%d" % c0)
             nc.sync.dma_start(raw[:], q_rows[:, :, c0 : c0 + w])
             q_raw.extend(raw[:, :, c : c + P] for c in range(0, w, P))
@@ -52,7 +52,7 @@ def tile_attend_sddmm_ts_kernel(tc, qT, kT, ts, offs, out):
         windows = []
         for m in range(NQ // P):
             window = keep.tile([P, T], F32, name="window%d" % m)
-            nc.vector.memset(window[:], 0.0)
+            nc.gpsimd.memset(window[:], 0.0)
             windows.append(window)
 
         ts_pool = keep.tile([P, T], F32, name="ts_pool")
@@ -67,7 +67,8 @@ def tile_attend_sddmm_ts_kernel(tc, qT, kT, ts, offs, out):
         q_codes, q_scales, q_grouped = {}, {}, {}
 
         def group_queries(m, copy):
-            grouped = keep.tile([P, P, PACK], BF16, name="q_grouped%d" % m, align_bytes=64)
+            tag = "q_codes%d" % (m - 2) if m >= 2 else "q_grouped%d" % m
+            grouped = keep.tile([P, P, PACK], BF16, name="q_grouped%d" % m, tag=tag, align_bytes=64)
             copy(grouped[:].rearrange("p (c i) t -> p c t i", i=4), q_raw[m].rearrange("p t (c i) -> p c t i", i=4))
             q_grouped[m] = grouped
 
@@ -81,7 +82,8 @@ def tile_attend_sddmm_ts_kernel(tc, qT, kT, ts, offs, out):
 
         def score(m, cols):
             if m not in scores:
-                scores[m] = keep.tile([P, N], F32, name="scores%d" % m)
+                tag = "q_raw%d" % ((m + 1) * P) if m in (1, 2) else "scores%d" % m
+                scores[m] = keep.tile([P, N], F32, name="scores%d" % m, tag=tag)
             acc = psum.tile([P, cols.stop - cols.start], F32, name="acc%d_%d" % (m, cols.start))
             nc.tensor.matmul_mx(
                 out=acc[:],
@@ -108,7 +110,6 @@ def tile_attend_sddmm_ts_kernel(tc, qT, kT, ts, offs, out):
         k_grouped = keep.tile([P, N, PACK], BF16, name="k_grouped", align_bytes=64)
         k_codes = keep.tile([P, N], U32, name="k_codes", align_bytes=64)
         k_scales = keep.tile([P, N], U8, name="k_scales", align_bytes=64)
-        ts_listed = keep.tile([P, N], F32, name="ts_listed")
         whole, first, second = slice(0, N), slice(0, half), slice(half, N)
 
         def quantize_keys(cols):
@@ -119,31 +120,31 @@ def tile_attend_sddmm_ts_kernel(tc, qT, kT, ts, offs, out):
             )
 
         nc.vector.tensor_copy(g01[:, 0, :], listed(k_pool[0], whole))
-        nc.vector.tensor_copy(ts_listed[:], listed(ts_pool, whole))
         nc.vector.tensor_copy(g01[:, 1, :], listed(k_pool[1], whole))
         nc.scalar.copy(k_grouped[:, :, 0:2], g01[:].rearrange("p t c -> p c t"))
         nc.vector.tensor_copy(g23[:, 0, :], listed(k_pool[2], whole))
         for cols in (first, second):
             nc.vector.tensor_copy(g23[:, 1, cols], listed(k_pool[3], cols))
-        for copy, cols in ((nc.scalar.copy, slice(0, 128)), (nc.vector.tensor_copy, slice(128, 256)), (nc.vector.tensor_copy, slice(256, 512))):
+        for copy, cols in ((nc.scalar.copy, first), (nc.vector.tensor_copy, second)):
             copy(k_grouped[:, cols, 2:4], g23[:, :, cols].rearrange("p t c -> p c t"))
         group_queries(0, nc.scalar.copy)
         group_queries(1, nc.scalar.copy)
         quantize_keys(first)
-        quantize_queries(0)
         quantize_keys(second)
+        quantize_queries(0)
         score(0, first)
         score(0, second)
+        ts_listed = keep.tile([P, N], F32, name="ts_listed", tag="q_grouped0", align_bytes=64)
+        nc.vector.tensor_copy(ts_listed[:], listed(ts_pool, whole))
         quantize_queries(1)
-        group_queries(2, nc.vector.tensor_copy)
-        place(0, first)
-        place(0, second)
+        place(0, whole)
         store(0)
+        group_queries(2, nc.scalar.copy)
         score(1, whole)
         quantize_queries(2)
-        group_queries(3, nc.scalar.copy)
         place(1, whole)
         store(1)
+        group_queries(3, nc.scalar.copy)
         score(2, whole)
         quantize_queries(3)
         place(2, whole)

@@ -1,7 +1,6 @@
 from contextlib import ExitStack
 
 import concourse.mybir as mybir
-from concourse.masks import make_identity
 
 D_FEAT, NQ, T, N = 512, 512, 1024, 512
 P = 128
@@ -23,7 +22,6 @@ def tile_attend_sddmm_ts_kernel(tc, qT, kT, ts, offs, out):
     q_rows = qT.rearrange("b (p t) q -> p (b t) q", t=PACK)
     out_rows = out.rearrange("b (m p) w -> p (b m) w", p=P)
     half = N // 2
-    per = T // P
 
     with ExitStack() as ctx:
         keep = ctx.enter_context(tc.tile_pool(name="keep", bufs=1))
@@ -31,8 +29,6 @@ def tile_attend_sddmm_ts_kernel(tc, qT, kT, ts, offs, out):
 
         offsets = keep.tile([P, N // 16], U16, name="offsets")
         nc.sync.dma_start(offsets[:], offs)
-        ts_cols = keep.tile([P, per], F32, name="ts_cols")
-        nc.scalar.dma_start(ts_cols[:], ts[0:1, :].rearrange("o (p j) -> (o p) j", j=per))
 
         k_pool = []
         for t in range(PACK):
@@ -40,14 +36,14 @@ def tile_attend_sddmm_ts_kernel(tc, qT, kT, ts, offs, out):
             nc.sync.dma_start(plane[:], k_rows[:, t, :])
             k_pool.append(plane)
 
+        ts_pool = keep.tile([P, T], F32, name="ts_pool")
         q_raw = []
-        for c0, w in ((0, 2 * P), (2 * P, P), (3 * P, P)):
+        for c0, w in ((0, P), (P, P), (2 * P, P), (3 * P, P)):
             raw = keep.tile([P, PACK, w], F32, name="q_raw%d" % c0)
             nc.sync.dma_start(raw[:], q_rows[:, :, c0 : c0 + w])
             q_raw.extend(raw[:, :, c : c + P] for c in range(0, w, P))
-
-        ident = keep.tile([P, P], F32, name="ident")
-        make_identity(nc, ident[:])
+            if c0 == P:
+                nc.sync.dma_start(ts_pool[:], ts)
 
         windows = []
         for m in range(NQ // P):
@@ -55,19 +51,10 @@ def tile_attend_sddmm_ts_kernel(tc, qT, kT, ts, offs, out):
             nc.gpsimd.memset(window[:], 0.0)
             windows.append(window)
 
-        ts_pool = keep.tile([P, T], F32, name="ts_pool")
-        ts_by_j = ts_pool[:].rearrange("p (n j) -> p n j", j=per)
-        for g in range(per // 4):
-            spread = psum.tile([P, 4, P], F32, name="spread%d" % g)
-            for j in range(4):
-                col = 4 * g + j
-                nc.tensor.transpose(spread[:, j, :], ts_cols[:, col : col + 1].to_broadcast([P, P]), ident[:])
-            nc.scalar.copy(ts_by_j[:, :, 4 * g : 4 * g + 4], spread[:].rearrange("p j n -> p n j"))
-
         q_codes, q_scales, q_grouped = {}, {}, {}
 
         def group_queries(m, copy):
-            tag = "q_codes%d" % (m - 2) if m >= 2 else "q_grouped%d" % m
+            tag = "q_codes0" if m >= 2 else "q_grouped%d" % m
             grouped = keep.tile([P, P, PACK], BF16, name="q_grouped%d" % m, tag=tag, align_bytes=64)
             copy(grouped[:].rearrange("p (c i) t -> p c t i", i=4), q_raw[m].rearrange("p t (c i) -> p c t i", i=4))
             q_grouped[m] = grouped
@@ -125,16 +112,20 @@ def tile_attend_sddmm_ts_kernel(tc, qT, kT, ts, offs, out):
         nc.vector.tensor_copy(g23[:, 0, :], listed(k_pool[2], whole))
         for cols in (first, second):
             nc.vector.tensor_copy(g23[:, 1, cols], listed(k_pool[3], cols))
-        for copy, cols in ((nc.scalar.copy, first), (nc.vector.tensor_copy, second)):
-            copy(k_grouped[:, cols, 2:4], g23[:, :, cols].rearrange("p t c -> p c t"))
+
+        def pair_up(cols):
+            nc.vector.tensor_copy(k_grouped[:, cols, 2:4], g23[:, :, cols].rearrange("p t c -> p c t"))
+
         group_queries(0, nc.scalar.copy)
         group_queries(1, nc.scalar.copy)
-        quantize_keys(first)
-        quantize_keys(second)
+        pair_up(first)
         quantize_queries(0)
+        pair_up(second)
+        quantize_keys(first)
         score(0, first)
+        quantize_keys(second)
         score(0, second)
-        ts_listed = keep.tile([P, N], F32, name="ts_listed", tag="q_grouped0", align_bytes=64)
+        ts_listed = keep.tile([P, N], F32, name="ts_listed")
         nc.vector.tensor_copy(ts_listed[:], listed(ts_pool, whole))
         quantize_queries(1)
         place(0, whole)

@@ -28,18 +28,19 @@ def tile_attend_sddmm_ts_kernel(tc, qT, kT, ts, offs, out):
         psum = ctx.enter_context(tc.psum_pool(name="psum", bufs=1))
 
         offsets = keep.tile([P, N // 16], U16, name="offsets")
-        nc.sync.dma_start(offsets[:], offs)
 
         k_pool = []
         for t in range(PACK):
             plane = keep.tile([P, T], F32, name="k_plane%d" % t)
             nc.sync.dma_start(plane[:], k_rows[:, t, :])
             k_pool.append(plane)
+            if t == 0:
+                nc.sync.dma_start(offsets[:], offs)
 
         ts_pool = keep.tile([P, T], F32, name="ts_pool")
         q_raw = []
         for c0, w in ((0, P), (P, P), (2 * P, P), (3 * P, P)):
-            raw = keep.tile([P, PACK, w], F32, name="q_raw%d" % c0)
+            raw = keep.tile([P, PACK, w], F32, name="q_raw%d" % c0, align_bytes=64)
             nc.sync.dma_start(raw[:], q_rows[:, :, c0 : c0 + w])
             q_raw.extend(raw[:, :, c : c + P] for c in range(0, w, P))
             if c0 == P:
@@ -48,13 +49,13 @@ def tile_attend_sddmm_ts_kernel(tc, qT, kT, ts, offs, out):
         windows = []
         for m in range(NQ // P):
             window = keep.tile([P, T], F32, name="window%d" % m)
-            nc.gpsimd.memset(window[:], 0.0)
+            nc.vector.memset(window[:], 0.0)
             windows.append(window)
 
         q_codes, q_scales, q_grouped = {}, {}, {}
 
         def group_queries(m, copy):
-            tag = "q_codes0" if m >= 2 else "q_grouped%d" % m
+            tag = ("g01", "q_raw0", "q_codes0", "q_codes0")[m]
             grouped = keep.tile([P, P, PACK], BF16, name="q_grouped%d" % m, tag=tag, align_bytes=64)
             copy(grouped[:].rearrange("p (c i) t -> p c t i", i=4), q_raw[m].rearrange("p t (c i) -> p c t i", i=4))
             q_grouped[m] = grouped
@@ -70,7 +71,7 @@ def tile_attend_sddmm_ts_kernel(tc, qT, kT, ts, offs, out):
         def score(m, cols):
             if m not in scores:
                 tag = "q_raw%d" % ((m + 1) * P) if m in (1, 2) else "scores%d" % m
-                scores[m] = keep.tile([P, N], F32, name="scores%d" % m, tag=tag)
+                scores[m] = keep.tile([P, N], F32, name="scores%d" % m, tag=tag, align_bytes=64)
             acc = psum.tile([P, cols.stop - cols.start], F32, name="acc%d_%d" % (m, cols.start))
             nc.tensor.matmul_mx(
                 out=acc[:],
@@ -92,7 +93,7 @@ def tile_attend_sddmm_ts_kernel(tc, qT, kT, ts, offs, out):
         def store(m):
             nc.sync.dma_start(out_rows[:, m, :], windows[m][:])
 
-        g01 = keep.tile([P, 2, N], F32, name="g01")
+        g01 = keep.tile([P, 2, N], F32, name="g01", align_bytes=64)
         g23 = keep.tile([P, 2, N], F32, name="g23")
         k_grouped = keep.tile([P, N, PACK], BF16, name="k_grouped", align_bytes=64)
         k_codes = keep.tile([P, N], U32, name="k_codes", align_bytes=64)

@@ -109,8 +109,9 @@ def tile_attend_sddmm_ts_kernel(tc, qT, kT, ts, offs, out):
 
         nc.vector.tensor_copy(g01[:, 0, :], listed(k_pool[0], whole))
         nc.vector.tensor_copy(g01[:, 1, :], listed(k_pool[1], whole))
-        nc.scalar.copy(k_grouped[:, :, 0:2], g01[:].rearrange("p t c -> p c t"))
+        nc.scalar.copy(k_grouped[:, first, 0:2], g01[:, :, first].rearrange("p t c -> p c t"))
         nc.vector.tensor_copy(g23[:, 0, :], listed(k_pool[2], whole))
+        nc.vector.tensor_copy(k_grouped[:, second, 0:2], g01[:, :, second].rearrange("p t c -> p c t"))
         for cols in (first, second):
             nc.vector.tensor_copy(g23[:, 1, cols], listed(k_pool[3], cols))
 

@@ -1,6 +1,7 @@
 from contextlib import ExitStack
 
 import concourse.mybir as mybir
+from concourse.masks import make_identity
 
 D_FEAT, NQ, T, N = 512, 512, 1024, 512
 P = 128
@@ -29,22 +30,24 @@ def tile_attend_sddmm_ts_kernel(tc, qT, kT, ts, offs, out):
 
         offsets = keep.tile([P, N // 16], U16, name="offsets")
 
+        ts_cols = keep.tile([P, T // P], F32, name="ts_cols", align_bytes=64)
+        nc.scalar.dma_start(ts_cols[:], ts[0:1, :].rearrange("o (p j) -> (o p) j", p=P))
+        ident = keep.tile([P, P], F32, name="ident")
+        make_identity(nc, ident[:])
+
         k_pool = []
         for t in range(PACK):
-            plane = keep.tile([P, T], F32, name="k_plane%d" % t)
+            plane = keep.tile([P, T], F32, name="k_plane%d" % t, align_bytes=64)
             nc.sync.dma_start(plane[:], k_rows[:, t, :])
             k_pool.append(plane)
             if t == 0:
                 nc.sync.dma_start(offsets[:], offs)
 
-        ts_pool = keep.tile([P, T], F32, name="ts_pool")
         q_raw = []
         for c0, w in ((0, P), (P, P), (2 * P, P), (3 * P, P)):
             raw = keep.tile([P, PACK, w], F32, name="q_raw%d" % c0, align_bytes=64)
             nc.sync.dma_start(raw[:], q_rows[:, :, c0 : c0 + w])
             q_raw.extend(raw[:, :, c : c + P] for c in range(0, w, P))
-            if c0 == P:
-                nc.sync.dma_start(ts_pool[:], ts)
 
         windows = []
         for m in range(NQ // P):
@@ -52,16 +55,25 @@ def tile_attend_sddmm_ts_kernel(tc, qT, kT, ts, offs, out):
             nc.vector.memset(window[:], 0.0)
             windows.append(window)
 
+        ts_pool = keep.tile([P, T], F32, name="ts_pool", align_bytes=64)
+        ts_by_col = ts_pool[:].rearrange("p (n j) -> p n j", n=P)
+        for h in range(2):
+            bank = psum.tile([P, 4, P], F32, name="ts_bank%d" % h)
+            for j in range(4):
+                nc.tensor.transpose(bank[:, j, :], ts_cols[:, 4 * h + j : 4 * h + j + 1].to_broadcast([P, P]), ident[:])
+            nc.scalar.copy(ts_by_col[:, :, 4 * h : 4 * h + 4], bank[:].rearrange("p j n -> p n j"))
+
         q_codes, q_scales, q_grouped = {}, {}, {}
 
         def group_queries(m, copy):
-            tag = ("g01", "q_raw0", "q_codes0", "q_codes0")[m]
+            tag = ("g01", "q_raw0", "k_plane3", "q_raw256")[m]
             grouped = keep.tile([P, P, PACK], BF16, name="q_grouped%d" % m, tag=tag, align_bytes=64)
             copy(grouped[:].rearrange("p (c i) t -> p c t i", i=4), q_raw[m].rearrange("p t (c i) -> p c t i", i=4))
             q_grouped[m] = grouped
 
         def quantize_queries(m):
-            codes = keep.tile([P, P], U32, name="q_codes%d" % m, align_bytes=64)
+            tag = ("k_plane3", "ts_pool", "q_codes2", "q_codes3")[m]
+            codes = keep.tile([P, P], U32, name="q_codes%d" % m, tag=tag, align_bytes=64)
             scales = keep.tile([P, P], U8, name="q_scales%d" % m, align_bytes=64)
             nc.vector.quantize_mx(out=codes[:].bitcast(FP8X4), scales=scales[:], in_=q_grouped[m][:].rearrange("p c t -> p (c t)"))
             q_codes[m], q_scales[m] = codes, scales
@@ -70,8 +82,7 @@ def tile_attend_sddmm_ts_kernel(tc, qT, kT, ts, offs, out):
 
         def score(m, cols):
             if m not in scores:
-                tag = "q_raw%d" % ((m + 1) * P) if m in (1, 2) else "scores%d" % m
-                scores[m] = keep.tile([P, N], F32, name="scores%d" % m, tag=tag, align_bytes=64)
+                scores[m] = keep.tile([P, N], F32, name="scores%d" % m, align_bytes=64)
             acc = psum.tile([P, cols.stop - cols.start], F32, name="acc%d_%d" % (m, cols.start))
             nc.tensor.matmul_mx(
                 out=acc[:],
@@ -94,8 +105,8 @@ def tile_attend_sddmm_ts_kernel(tc, qT, kT, ts, offs, out):
             nc.sync.dma_start(out_rows[:, m, :], windows[m][:])
 
         g01 = keep.tile([P, 2, N], F32, name="g01", align_bytes=64)
-        g23 = keep.tile([P, 2, N], F32, name="g23")
-        k_grouped = keep.tile([P, N, PACK], BF16, name="k_grouped", align_bytes=64)
+        ts_listed = keep.tile([P, N], F32, name="ts_listed")
+        k_grouped = keep.tile([P, N, PACK], BF16, name="k_grouped", tag="ts_cols", align_bytes=64)
         k_codes = keep.tile([P, N], U32, name="k_codes", align_bytes=64)
         k_scales = keep.tile([P, N], U8, name="k_scales", align_bytes=64)
         whole, first, second = slice(0, N), slice(0, half), slice(half, N)
@@ -109,9 +120,10 @@ def tile_attend_sddmm_ts_kernel(tc, qT, kT, ts, offs, out):
 
         nc.vector.tensor_copy(g01[:, 0, :], listed(k_pool[0], whole))
         nc.vector.tensor_copy(g01[:, 1, :], listed(k_pool[1], whole))
-        nc.scalar.copy(k_grouped[:, first, 0:2], g01[:, :, first].rearrange("p t c -> p c t"))
+        nc.scalar.copy(k_grouped[:, :, 0:2], g01[:].rearrange("p t c -> p c t"))
+        nc.vector.tensor_copy(ts_listed[:], listed(ts_pool, whole))
+        g23 = keep.tile([P, 2, N], F32, name="g23", tag="ts_pool", align_bytes=64)
         nc.vector.tensor_copy(g23[:, 0, :], listed(k_pool[2], whole))
-        nc.vector.tensor_copy(k_grouped[:, second, 0:2], g01[:, :, second].rearrange("p t c -> p c t"))
         for cols in (first, second):
             nc.vector.tensor_copy(g23[:, 1, cols], listed(k_pool[3], cols))
 
@@ -121,14 +133,12 @@ def tile_attend_sddmm_ts_kernel(tc, qT, kT, ts, offs, out):
         group_queries(0, nc.scalar.copy)
         group_queries(1, nc.scalar.copy)
         pair_up(first)
-        quantize_queries(0)
         pair_up(second)
         quantize_keys(first)
+        quantize_queries(0)
         score(0, first)
         quantize_keys(second)
         score(0, second)
-        ts_listed = keep.tile([P, N], F32, name="ts_listed")
-        nc.vector.tensor_copy(ts_listed[:], listed(ts_pool, whole))
         quantize_queries(1)
         place(0, whole)
         store(0)

@@ -66,7 +66,7 @@ def tile_attend_sddmm_ts_kernel(tc, qT, kT, ts, offs, out):
         q_codes, q_scales, q_grouped = {}, {}, {}
 
         def group_queries(m, copy):
-            tag = ("g01", "q_raw0", "k_plane3", "q_raw256")[m]
+            tag = ("g01", "q_raw0", "g01", "k_plane3")[m]
             grouped = keep.tile([P, P, PACK], BF16, name="q_grouped%d" % m, tag=tag, align_bytes=64)
             copy(grouped[:].rearrange("p (c i) t -> p c t i", i=4), q_raw[m].rearrange("p t (c i) -> p c t i", i=4))
             q_grouped[m] = grouped
@@ -140,18 +140,13 @@ def tile_attend_sddmm_ts_kernel(tc, qT, kT, ts, offs, out):
         quantize_keys(second)
         score(0, second)
         quantize_queries(1)
+        group_queries(2, nc.vector.tensor_copy)
+        quantize_queries(2)
         place(0, whole)
         store(0)
-        group_queries(2, nc.scalar.copy)
-        score(1, whole)
-        quantize_queries(2)
-        place(1, whole)
-        store(1)
         group_queries(3, nc.scalar.copy)
-        score(2, whole)
         quantize_queries(3)
-        place(2, whole)
-        store(2)
-        score(3, whole)
-        place(3, whole)
-        store(3)
+        for m in (1, 2, 3):
+            score(m, whole)
+            place(m, whole)
+            store(m)

@@ -1,20 +1,23 @@
 from contextlib import ExitStack
 
 import concourse.mybir as mybir
-from concourse.masks import make_identity
 
 D_FEAT, NQ, T, N = 512, 512, 1024, 512
 P = 128
 PACK = 4
+QUAD = 32
 FLOPS = 2 * D_FEAT * NQ * N
 
 F32 = mybir.dt.float32
 BF16 = mybir.dt.bfloat16
+I32 = mybir.dt.int32
 U32 = mybir.dt.uint32
 U16 = mybir.dt.uint16
 U8 = mybir.dt.uint8
 FP8X4 = mybir.dt.float8_e4m3fn_x4
 MULT = mybir.AluOpType.mult
+ADD = mybir.AluOpType.add
+IS_EQUAL = mybir.AluOpType.is_equal
 
 
 def tile_attend_sddmm_ts_kernel(tc, qT, kT, ts, offs, out):
@@ -23,31 +26,45 @@ def tile_attend_sddmm_ts_kernel(tc, qT, kT, ts, offs, out):
     q_rows = qT.rearrange("b (p t) q -> p (b t) q", t=PACK)
     out_rows = out.rearrange("b (m p) w -> p (b m) w", p=P)
     half = N // 2
+    whole, halves = slice(0, N), (slice(0, half), slice(half, N))
 
     with ExitStack() as ctx:
         keep = ctx.enter_context(tc.tile_pool(name="keep", bufs=1))
         psum = ctx.enter_context(tc.psum_pool(name="psum", bufs=1))
 
+        def sb(shape, dtype, name, tag=None):
+            return keep.tile(shape, dtype, name=name, tag=tag or name, align_bytes=64)
+
         offsets = keep.tile([P, N // 16], U16, name="offsets")
 
-        ts_cols = keep.tile([P, T // P], F32, name="ts_cols", align_bytes=64)
+        ts_cols = sb([P, T // P], F32, "ts_cols")
         nc.scalar.dma_start(ts_cols[:], ts[0:1, :].rearrange("o (p j) -> (o p) j", p=P))
-        ident = keep.tile([P, P], F32, name="ident")
-        make_identity(nc, ident[:])
 
         k_pool = []
         for t in range(PACK):
-            plane = keep.tile([P, T], F32, name="k_plane%d" % t, align_bytes=64)
+            plane = sb([P, T], F32, "k_plane%d" % t)
             nc.sync.dma_start(plane[:], k_rows[:, t, :])
             k_pool.append(plane)
             if t == 0:
                 nc.sync.dma_start(offsets[:], offs)
 
         q_raw = []
-        for c0, w in ((0, P), (P, P), (2 * P, P), (3 * P, P)):
-            raw = keep.tile([P, PACK, w], F32, name="q_raw%d" % c0, align_bytes=64)
-            nc.sync.dma_start(raw[:], q_rows[:, :, c0 : c0 + w])
-            q_raw.extend(raw[:, :, c : c + P] for c in range(0, w, P))
+        for m in range(NQ // P):
+            raw = sb([P, PACK, P], F32, "q_raw%d" % m)
+            nc.sync.dma_start(raw[:], q_rows[:, :, m * P : (m + 1) * P])
+            q_raw.append(raw)
+
+        ones = sb([P, QUAD], F32, "ones")
+        col_no = sb([P, QUAD], F32, "col_no")
+        row_no = sb([P, QUAD], F32, "row_no")
+        ident = sb([P, P], F32, "ident")
+        nc.vector.memset(ones[:], 1.0)
+        nc.vector.memset(ident[:], 0.0)
+        nc.vector.tensor_tensor_scan(col_no[:], ones[:], ones[:], 0.0, MULT, ADD)
+        nc.vector.transpose(row_no[:], col_no[:])
+        for g in range(P // QUAD):
+            rows = slice(g * QUAD, (g + 1) * QUAD)
+            nc.vector.tensor_tensor(ident[rows, rows], col_no[rows, :], row_no[rows, :], IS_EQUAL)
 
         windows = []
         for m in range(NQ // P):
@@ -55,7 +72,7 @@ def tile_attend_sddmm_ts_kernel(tc, qT, kT, ts, offs, out):
             nc.vector.memset(window[:], 0.0)
             windows.append(window)
 
-        ts_pool = keep.tile([P, T], F32, name="ts_pool", align_bytes=64)
+        ts_pool = sb([P, T], F32, "ts_pool")
         ts_by_col = ts_pool[:].rearrange("p (n j) -> p n j", n=P)
         for h in range(2):
             bank = psum.tile([P, 4, P], F32, name="ts_bank%d" % h)
@@ -63,26 +80,23 @@ def tile_attend_sddmm_ts_kernel(tc, qT, kT, ts, offs, out):
                 nc.tensor.transpose(bank[:, j, :], ts_cols[:, 4 * h + j : 4 * h + j + 1].to_broadcast([P, P]), ident[:])
             nc.scalar.copy(ts_by_col[:, :, 4 * h : 4 * h + 4], bank[:].rearrange("p j n -> p n j"))
 
-        q_codes, q_scales, q_grouped = {}, {}, {}
+        def listed(tile, cols):
+            return tile[:].indirect(offsets[:, cols.start // 16 : cols.stop // 16])
 
-        def group_queries(m, copy):
-            tag = ("g01", "q_raw0", "g01", "k_plane3")[m]
-            grouped = keep.tile([P, P, PACK], BF16, name="q_grouped%d" % m, tag=tag, align_bytes=64)
-            copy(grouped[:].rearrange("p (c i) t -> p c t i", i=4), q_raw[m].rearrange("p t (c i) -> p c t i", i=4))
+        q_codes, q_scales, q_grouped, scores = {}, {}, {}, {}
+
+        def group_queries(m, copy, tag=None):
+            grouped = sb([P, P, PACK], BF16, "q_grouped%d" % m, tag)
+            copy(grouped[:].rearrange("p (c i) t -> p c t i", i=4), q_raw[m][:].rearrange("p t (c i) -> p c t i", i=4))
             q_grouped[m] = grouped
 
         def quantize_queries(m):
-            tag = ("k_plane3", "ts_pool", "q_codes2", "q_codes3")[m]
-            codes = keep.tile([P, P], U32, name="q_codes%d" % m, tag=tag, align_bytes=64)
-            scales = keep.tile([P, P], U8, name="q_scales%d" % m, align_bytes=64)
+            codes = sb([P, P], U32, "q_codes%d" % m)
+            scales = sb([P, P], U8, "q_scales%d" % m)
             nc.vector.quantize_mx(out=codes[:].bitcast(FP8X4), scales=scales[:], in_=q_grouped[m][:].rearrange("p c t -> p (c t)"))
             q_codes[m], q_scales[m] = codes, scales
 
-        scores = {}
-
-        def score(m, cols):
-            if m not in scores:
-                scores[m] = keep.tile([P, N], F32, name="scores%d" % m, align_bytes=64)
+        def multiply(m, cols):
             acc = psum.tile([P, cols.stop - cols.start], F32, name="acc%d_%d" % (m, cols.start))
             nc.tensor.matmul_mx(
                 out=acc[:],
@@ -93,10 +107,12 @@ def tile_attend_sddmm_ts_kernel(tc, qT, kT, ts, offs, out):
                 start=True,
                 stop=True,
             )
-            nc.scalar.copy(scores[m][:, cols], acc[:])
+            return acc
 
-        def listed(tile, cols):
-            return tile[:].indirect(offsets[:, cols.start // 16 : cols.stop // 16])
+        def score(m, cols):
+            if m not in scores:
+                scores[m] = sb([P, N], F32, "scores%d" % m)
+            nc.scalar.copy(scores[m][:, cols], multiply(m, cols)[:])
 
         def place(m, cols):
             nc.vector.tensor_tensor(listed(windows[m], cols), scores[m][:, cols], ts_listed[:, cols], MULT)
@@ -104,49 +120,60 @@ def tile_attend_sddmm_ts_kernel(tc, qT, kT, ts, offs, out):
         def store(m):
             nc.sync.dma_start(out_rows[:, m, :], windows[m][:])
 
-        g01 = keep.tile([P, 2, N], F32, name="g01", align_bytes=64)
-        ts_listed = keep.tile([P, N], F32, name="ts_listed")
-        k_grouped = keep.tile([P, N, PACK], BF16, name="k_grouped", tag="ts_cols", align_bytes=64)
-        k_codes = keep.tile([P, N], U32, name="k_codes", align_bytes=64)
-        k_scales = keep.tile([P, N], U8, name="k_scales", align_bytes=64)
-        whole, first, second = slice(0, N), slice(0, half), slice(half, N)
+        shared = sb([P, N + half], F32, "shared")
+        ts_listed = shared[:, 0:N]
+        pairs = [
+            sb([P, 2, half, 2], BF16, "pairs0")[:],
+            shared[:, half:].bitcast(BF16).rearrange("p (u c e) -> p u c e", u=2, e=2),
+        ]
+        k_grouped = [sb([P, half, PACK], BF16, "k_grouped%d" % h) for h in range(2)]
+        k_codes = sb([P, N], U32, "k_codes")
+        k_scales = sb([P, N], U8, "k_scales")
 
-        def quantize_keys(cols):
+        def gather_plane(t):
+            for h in range(2):
+                nc.vector.tensor_copy(pairs[h][:, t // 2, :, t % 2], listed(k_pool[t], halves[h]))
+
+        def weave(h, copy, word):
+            words = pairs[h].rearrange("p u c e -> p u (c e)").bitcast(word)
+            copy(k_grouped[h][:].bitcast(word), words.rearrange("p u c -> p c u"))
+
+        def quantize_keys(h):
             nc.vector.quantize_mx(
-                out=k_codes[:, cols].bitcast(FP8X4),
-                scales=k_scales[:, cols],
-                in_=k_grouped[:, cols, :].rearrange("p c t -> p (c t)"),
+                out=k_codes[:, halves[h]].bitcast(FP8X4),
+                scales=k_scales[:, halves[h]],
+                in_=k_grouped[h][:].rearrange("p c t -> p (c t)"),
             )
 
-        nc.vector.tensor_copy(g01[:, 0, :], listed(k_pool[0], whole))
-        nc.vector.tensor_copy(g01[:, 1, :], listed(k_pool[1], whole))
-        nc.scalar.copy(k_grouped[:, :, 0:2], g01[:].rearrange("p t c -> p c t"))
-        nc.vector.tensor_copy(ts_listed[:], listed(ts_pool, whole))
-        g23 = keep.tile([P, 2, N], F32, name="g23", tag="ts_pool", align_bytes=64)
-        nc.vector.tensor_copy(g23[:, 0, :], listed(k_pool[2], whole))
-        for cols in (first, second):
-            nc.vector.tensor_copy(g23[:, 1, cols], listed(k_pool[3], cols))
-
-        def pair_up(cols):
-            nc.vector.tensor_copy(k_grouped[:, cols, 2:4], g23[:, :, cols].rearrange("p t c -> p c t"))
-
-        group_queries(0, nc.scalar.copy)
+        gather_plane(0)
+        gather_plane(1)
+        nc.vector.tensor_copy(ts_listed[:, halves[0]], listed(ts_pool, halves[0]))
+        gather_plane(2)
+        gather_plane(3)
+        weave(0, nc.vector.tensor_copy, I32)
+        weave(1, nc.scalar.copy, U32)
+        group_queries(0, nc.vector.tensor_copy)
         group_queries(1, nc.scalar.copy)
-        pair_up(first)
-        pair_up(second)
-        quantize_keys(first)
+        quantize_keys(0)
         quantize_queries(0)
-        score(0, first)
-        quantize_keys(second)
-        score(0, second)
+        score(0, halves[0])
+        quantize_keys(1)
+        score(0, halves[1])
+        nc.vector.tensor_copy(ts_listed[:, halves[1]], listed(ts_pool, halves[1]))
         quantize_queries(1)
-        group_queries(2, nc.vector.tensor_copy)
+        group_queries(2, nc.vector.tensor_copy, "q_raw1")
+        place(0, halves[0])
         quantize_queries(2)
-        place(0, whole)
+        place(0, halves[1])
         store(0)
-        group_queries(3, nc.scalar.copy)
+        score(1, whole)
+        group_queries(3, nc.scalar.copy, "q_codes1")
+        place(1, whole)
+        store(1)
+        score(2, whole)
         quantize_queries(3)
-        for m in (1, 2, 3):
-            score(m, whole)
-            place(m, whole)
-            store(m)
+        place(2, whole)
+        store(2)
+        score(3, whole)
+        place(3, whole)
+        store(3)

@@ -49,10 +49,13 @@ def tile_attend_sddmm_ts_kernel(tc, qT, kT, ts, offs, out):
                 nc.sync.dma_start(offsets[:], offs)
 
         q_raw = []
-        for m in range(NQ // P):
-            raw = sb([P, PACK, P], F32, "q_raw%d" % m)
-            nc.sync.dma_start(raw[:], q_rows[:, :, m * P : (m + 1) * P])
-            q_raw.append(raw)
+        shared = sb([P, half + N - P + PACK * 2 * P], F32, "shared")
+        ts_listed = shared[:, half : half + N]
+        raws = [sb([P, PACK, P], F32, "q_raw%d" % m)[:] for m in range(2)]
+        raws.append(shared[:, half + N - P :].rearrange("p (t c) -> p t c", t=PACK))
+        for raw, first, blocks in zip(raws, (0, 1, 2), (1, 1, 2)):
+            nc.sync.dma_start(raw, q_rows[:, :, first * P : (first + blocks) * P])
+            q_raw.extend(raw[:, :, b * P : (b + 1) * P] for b in range(blocks))
 
         ones = sb([P, QUAD], F32, "ones")
         col_no = sb([P, QUAD], F32, "col_no")
@@ -87,11 +90,11 @@ def tile_attend_sddmm_ts_kernel(tc, qT, kT, ts, offs, out):
 
         def group_queries(m, copy, tag=None):
             grouped = sb([P, P, PACK], BF16, "q_grouped%d" % m, tag)
-            copy(grouped[:].rearrange("p (c i) t -> p c t i", i=4), q_raw[m][:].rearrange("p t (c i) -> p c t i", i=4))
+            copy(grouped[:].rearrange("p (c i) t -> p c t i", i=4), q_raw[m].rearrange("p t (c i) -> p c t i", i=4))
             q_grouped[m] = grouped
 
-        def quantize_queries(m):
-            codes = sb([P, P], U32, "q_codes%d" % m)
+        def quantize_queries(m, tag=None):
+            codes = sb([P, P], U32, "q_codes%d" % m, tag)
             scales = sb([P, P], U8, "q_scales%d" % m)
             nc.vector.quantize_mx(out=codes[:].bitcast(FP8X4), scales=scales[:], in_=q_grouped[m][:].rearrange("p c t -> p (c t)"))
             q_codes[m], q_scales[m] = codes, scales
@@ -120,11 +123,9 @@ def tile_attend_sddmm_ts_kernel(tc, qT, kT, ts, offs, out):
         def store(m):
             nc.sync.dma_start(out_rows[:, m, :], windows[m][:])
 
-        shared = sb([P, N + half], F32, "shared")
-        ts_listed = shared[:, 0:N]
         pairs = [
             sb([P, 2, half, 2], BF16, "pairs0")[:],
-            shared[:, half:].bitcast(BF16).rearrange("p (u c e) -> p u c e", u=2, e=2),
+            shared[:, 0:N].bitcast(BF16).rearrange("p (u c e) -> p u c e", u=2, e=2),
         ]
         k_grouped = [sb([P, half, PACK], BF16, "k_grouped%d" % h) for h in range(2)]
         k_codes = sb([P, N], U32, "k_codes")
@@ -133,6 +134,9 @@ def tile_attend_sddmm_ts_kernel(tc, qT, kT, ts, offs, out):
         def gather_plane(t):
             for h in range(2):
                 nc.vector.tensor_copy(pairs[h][:, t // 2, :, t % 2], listed(k_pool[t], halves[h]))
+
+        def gather_scales(cols):
+            nc.vector.tensor_copy(ts_listed[:, cols], listed(ts_pool, cols))
 
         def weave(h, copy, word):
             words = pairs[h].rearrange("p u c e -> p u (c e)").bitcast(word)
@@ -147,7 +151,7 @@ def tile_attend_sddmm_ts_kernel(tc, qT, kT, ts, offs, out):
 
         gather_plane(0)
         gather_plane(1)
-        nc.vector.tensor_copy(ts_listed[:, halves[0]], listed(ts_pool, halves[0]))
+        gather_scales(slice(half, N - P))
         gather_plane(2)
         gather_plane(3)
         weave(0, nc.vector.tensor_copy, I32)
@@ -159,21 +163,16 @@ def tile_attend_sddmm_ts_kernel(tc, qT, kT, ts, offs, out):
         score(0, halves[0])
         quantize_keys(1)
         score(0, halves[1])
-        nc.vector.tensor_copy(ts_listed[:, halves[1]], listed(ts_pool, halves[1]))
+        gather_scales(halves[0])
         quantize_queries(1)
         group_queries(2, nc.vector.tensor_copy, "q_raw1")
-        place(0, halves[0])
+        gather_scales(slice(N - P, N))
         quantize_queries(2)
-        place(0, halves[1])
+        place(0, whole)
         store(0)
-        score(1, whole)
-        group_queries(3, nc.scalar.copy, "q_codes1")
-        place(1, whole)
-        store(1)
-        score(2, whole)
-        quantize_queries(3)
-        place(2, whole)
-        store(2)
-        score(3, whole)
-        place(3, whole)
-        store(3)
+        group_queries(3, nc.scalar.copy, "q_codes0")
+        quantize_queries(3, "ts_pool")
+        for m in (1, 2, 3):
+            score(m, whole)
+            place(m, whole)
+            store(m)

@@ -49,10 +49,10 @@ def tile_attend_sddmm_ts_kernel(tc, qT, kT, ts, offs, out):
                 nc.sync.dma_start(offsets[:], offs)
 
         q_raw = []
-        shared = sb([P, half + N - P + PACK * 2 * P], F32, "shared")
+        shared = sb([P, half + N - P // 2 + PACK * 2 * P], F32, "shared")
         ts_listed = shared[:, half : half + N]
         raws = [sb([P, PACK, P], F32, "q_raw%d" % m)[:] for m in range(2)]
-        raws.append(shared[:, half + N - P :].rearrange("p (t c) -> p t c", t=PACK))
+        raws.append(shared[:, half + N - P // 2 :].rearrange("p (t c) -> p t c", t=PACK))
         for raw, first, blocks in zip(raws, (0, 1, 2), (1, 1, 2)):
             nc.sync.dma_start(raw, q_rows[:, :, first * P : (first + blocks) * P])
             q_raw.extend(raw[:, :, b * P : (b + 1) * P] for b in range(blocks))
@@ -88,9 +88,14 @@ def tile_attend_sddmm_ts_kernel(tc, qT, kT, ts, offs, out):
 
         q_codes, q_scales, q_grouped, scores = {}, {}, {}, {}
 
-        def group_queries(m, copy, tag=None):
+        def group_queries(m, copy, tag=None, pieces=1):
             grouped = sb([P, P, PACK], BF16, "q_grouped%d" % m, tag)
-            copy(grouped[:].rearrange("p (c i) t -> p c t i", i=4), q_raw[m].rearrange("p t (c i) -> p c t i", i=4))
+            for c in range(0, P, P // pieces):
+                cols = slice(c, c + P // pieces)
+                copy(
+                    grouped[:, cols, :].rearrange("p (c i) t -> p c t i", i=4),
+                    q_raw[m][:, :, cols].rearrange("p t (c i) -> p c t i", i=4),
+                )
             q_grouped[m] = grouped
 
         def quantize_queries(m, tag=None):
@@ -154,7 +159,7 @@ def tile_attend_sddmm_ts_kernel(tc, qT, kT, ts, offs, out):
         gather_scales(slice(half, N - P))
         gather_plane(2)
         gather_plane(3)
-        weave(0, nc.vector.tensor_copy, I32)
+        weave(0, nc.scalar.copy, U32)
         weave(1, nc.scalar.copy, U32)
         group_queries(0, nc.vector.tensor_copy)
         group_queries(1, nc.scalar.copy)
@@ -165,7 +170,7 @@ def tile_attend_sddmm_ts_kernel(tc, qT, kT, ts, offs, out):
         score(0, halves[1])
         gather_scales(halves[0])
         quantize_queries(1)
-        group_queries(2, nc.vector.tensor_copy, "q_raw1")
+        group_queries(2, nc.vector.tensor_copy, pieces=2)
         gather_scales(slice(N - P, N))
         quantize_queries(2)
         place(0, whole)

@@ -49,25 +49,27 @@ def tile_attend_sddmm_ts_kernel(tc, qT, kT, ts, offs, out):
                 nc.sync.dma_start(offsets[:], offs)
 
         q_raw = []
-        shared = sb([P, half + N - P // 2 + PACK * 2 * P], F32, "shared")
-        ts_listed = shared[:, half : half + N]
+        shared = sb([P, N - P // 2 + PACK * 2 * P], F32, "shared")
+        ts_listed = shared[:, 0:N]
         raws = [sb([P, PACK, P], F32, "q_raw%d" % m)[:] for m in range(2)]
-        raws.append(shared[:, half + N - P // 2 :].rearrange("p (t c) -> p t c", t=PACK))
+        raws.append(shared[:, N - P // 2 :].rearrange("p (t c) -> p t c", t=PACK))
         for raw, first, blocks in zip(raws, (0, 1, 2), (1, 1, 2)):
             nc.sync.dma_start(raw, q_rows[:, :, first * P : (first + blocks) * P])
             q_raw.extend(raw[:, :, b * P : (b + 1) * P] for b in range(blocks))
 
-        ones = sb([P, QUAD], F32, "ones")
-        col_no = sb([P, QUAD], F32, "col_no")
-        row_no = sb([P, QUAD], F32, "row_no")
+        ones = sb([P, P], F32, "ones")
+        col_no = sb([P, P], F32, "col_no")
+        row_in_quad = sb([P, QUAD], F32, "row_in_quad")
+        quad_start = sb([P, 1], F32, "quad_start")
         ident = sb([P, P], F32, "ident")
-        nc.vector.memset(ones[:], 1.0)
-        nc.vector.memset(ident[:], 0.0)
-        nc.vector.tensor_tensor_scan(col_no[:], ones[:], ones[:], 0.0, MULT, ADD)
-        nc.vector.transpose(row_no[:], col_no[:])
         for g in range(P // QUAD):
-            rows = slice(g * QUAD, (g + 1) * QUAD)
-            nc.vector.tensor_tensor(ident[rows, rows], col_no[rows, :], row_no[rows, :], IS_EQUAL)
+            nc.gpsimd.memset(quad_start[g * QUAD : (g + 1) * QUAD, :], float(-g * QUAD))
+        nc.vector.memset(ones[:], 1.0)
+        warm = sb([P, 1], F32, "warm")
+        nc.scalar.copy(warm[:], ones[:, 0:1])
+        nc.vector.tensor_tensor_scan(col_no[:], ones[:], ones[:], 0.0, MULT, ADD)
+        nc.vector.transpose(row_in_quad[:], col_no[:, 0:QUAD])
+        nc.vector.tensor_scalar(ident[:], col_no[:], quad_start[:], row_in_quad[:, 0:1], ADD, IS_EQUAL)
 
         windows = []
         for m in range(NQ // P):
@@ -128,10 +130,7 @@ def tile_attend_sddmm_ts_kernel(tc, qT, kT, ts, offs, out):
         def store(m):
             nc.sync.dma_start(out_rows[:, m, :], windows[m][:])
 
-        pairs = [
-            sb([P, 2, half, 2], BF16, "pairs0")[:],
-            shared[:, 0:N].bitcast(BF16).rearrange("p (u c e) -> p u c e", u=2, e=2),
-        ]
+        pairs = [sb([P, 2, half, 2], BF16, "pairs%d" % h)[:] for h in range(2)]
         k_grouped = [sb([P, half, PACK], BF16, "k_grouped%d" % h) for h in range(2)]
         k_codes = sb([P, N], U32, "k_codes")
         k_scales = sb([P, N], U8, "k_scales")
@@ -156,7 +155,7 @@ def tile_attend_sddmm_ts_kernel(tc, qT, kT, ts, offs, out):
 
         gather_plane(0)
         gather_plane(1)
-        gather_scales(slice(half, N - P))
+        gather_scales(slice(0, N - P))
         gather_plane(2)
         gather_plane(3)
         weave(0, nc.scalar.copy, U32)
@@ -168,7 +167,6 @@ def tile_attend_sddmm_ts_kernel(tc, qT, kT, ts, offs, out):
         score(0, halves[0])
         quantize_keys(1)
         score(0, halves[1])
-        gather_scales(halves[0])
         quantize_queries(1)
         group_queries(2, nc.vector.tensor_copy, pieces=2)
         gather_scales(slice(N - P, N))

@@ -27,6 +27,7 @@ def tile_attend_sddmm_ts_kernel(tc, qT, kT, ts, offs, out):
     out_rows = out.rearrange("b (m p) w -> p (b m) w", p=P)
     half = N // 2
     whole, halves = slice(0, N), (slice(0, half), slice(half, N))
+    quarters = [slice(c, c + P) for c in range(0, N, P)]
 
     with ExitStack() as ctx:
         keep = ctx.enter_context(tc.tile_pool(name="keep", bufs=1))
@@ -49,13 +50,17 @@ def tile_attend_sddmm_ts_kernel(tc, qT, kT, ts, offs, out):
                 nc.sync.dma_start(offsets[:], offs)
 
         q_raw = []
-        shared = sb([P, N - P // 2 + PACK * 2 * P], F32, "shared")
-        ts_listed = shared[:, 0:N]
-        raws = [sb([P, PACK, P], F32, "q_raw%d" % m)[:] for m in range(2)]
-        raws.append(shared[:, N - P // 2 :].rearrange("p (t c) -> p t c", t=PACK))
-        for raw, first, blocks in zip(raws, (0, 1, 2), (1, 1, 2)):
-            nc.sync.dma_start(raw, q_rows[:, :, first * P : (first + blocks) * P])
-            q_raw.extend(raw[:, :, b * P : (b + 1) * P] for b in range(blocks))
+        ts_at = 2 * N - half
+        raw_at = ts_at + N - P // 2
+        shared = sb([P, raw_at + PACK * P], F32, "shared")
+        ts_listed = shared[:, ts_at : ts_at + N]
+        for m in range(NQ // P):
+            if m == 2:
+                raw = shared[:, raw_at:].rearrange("p (t c) -> p t c", t=PACK)
+            else:
+                raw = sb([P, PACK, P], F32, "q_raw%d" % m)[:]
+            nc.sync.dma_start(raw, q_rows[:, :, m * P : (m + 1) * P])
+            q_raw.append(raw)
 
         ones = sb([P, P], F32, "ones")
         col_no = sb([P, P], F32, "col_no")
@@ -65,8 +70,6 @@ def tile_attend_sddmm_ts_kernel(tc, qT, kT, ts, offs, out):
         for g in range(P // QUAD):
             nc.gpsimd.memset(quad_start[g * QUAD : (g + 1) * QUAD, :], float(-g * QUAD))
         nc.vector.memset(ones[:], 1.0)
-        warm = sb([P, 1], F32, "warm")
-        nc.scalar.copy(warm[:], ones[:, 0:1])
         nc.vector.tensor_tensor_scan(col_no[:], ones[:], ones[:], 0.0, MULT, ADD)
         nc.vector.transpose(row_in_quad[:], col_no[:, 0:QUAD])
         nc.vector.tensor_scalar(ident[:], col_no[:], quad_start[:], row_in_quad[:, 0:1], ADD, IS_EQUAL)
@@ -106,23 +109,21 @@ def tile_attend_sddmm_ts_kernel(tc, qT, kT, ts, offs, out):
             nc.vector.quantize_mx(out=codes[:].bitcast(FP8X4), scales=scales[:], in_=q_grouped[m][:].rearrange("p c t -> p (c t)"))
             q_codes[m], q_scales[m] = codes, scales
 
-        def multiply(m, cols):
-            acc = psum.tile([P, cols.stop - cols.start], F32, name="acc%d_%d" % (m, cols.start))
-            nc.tensor.matmul_mx(
-                out=acc[:],
-                lhsT=q_codes[m][:].bitcast(FP8X4),
-                lhsT_scale=q_scales[m][:],
-                rhs=k_codes[:, cols].bitcast(FP8X4),
-                rhs_scale=k_scales[:, cols],
-                start=True,
-                stop=True,
-            )
-            return acc
-
-        def score(m, cols):
+        def score(m, cols, passes):
             if m not in scores:
                 scores[m] = sb([P, N], F32, "scores%d" % m)
-            nc.scalar.copy(scores[m][:, cols], multiply(m, cols)[:])
+            acc = psum.tile([P, cols.stop - cols.start], F32, name="acc%d_%d" % (m, cols.start))
+            for part in passes:
+                nc.tensor.matmul_mx(
+                    out=acc[:, part.start - cols.start : part.stop - cols.start],
+                    lhsT=q_codes[m][:].bitcast(FP8X4),
+                    lhsT_scale=q_scales[m][:],
+                    rhs=k_codes[:, part].bitcast(FP8X4),
+                    rhs_scale=k_scales[:, part],
+                    start=True,
+                    stop=True,
+                )
+            nc.scalar.copy(scores[m][:, cols], acc[:])
 
         def place(m, cols):
             nc.vector.tensor_tensor(listed(windows[m], cols), scores[m][:, cols], ts_listed[:, cols], MULT)
@@ -130,52 +131,56 @@ def tile_attend_sddmm_ts_kernel(tc, qT, kT, ts, offs, out):
         def store(m):
             nc.sync.dma_start(out_rows[:, m, :], windows[m][:])
 
-        pairs = [sb([P, 2, half, 2], BF16, "pairs%d" % h)[:] for h in range(2)]
-        k_grouped = [sb([P, half, PACK], BF16, "k_grouped%d" % h) for h in range(2)]
+        pairs = shared[:, 0 : 2 * N].bitcast(BF16).rearrange("p (u c e) -> p u c e", u=2, e=2)
+        pair_words = shared[:, 0 : 2 * N].bitcast(U32).rearrange("p (u c) -> p c u", u=2)
+        k_grouped = [sb([P, P, PACK], BF16, "k_grouped%d" % c) for c in range(4)]
         k_codes = sb([P, N], U32, "k_codes")
         k_scales = sb([P, N], U8, "k_scales")
 
-        def gather_plane(t):
-            for h in range(2):
-                nc.vector.tensor_copy(pairs[h][:, t // 2, :, t % 2], listed(k_pool[t], halves[h]))
+        def gather_plane(t, pieces):
+            for cols in pieces:
+                nc.vector.tensor_copy(pairs[:, t // 2, cols, t % 2], listed(k_pool[t], cols))
 
         def gather_scales(cols):
             nc.vector.tensor_copy(ts_listed[:, cols], listed(ts_pool, cols))
 
-        def weave(h, copy, word):
-            words = pairs[h].rearrange("p u c e -> p u (c e)").bitcast(word)
-            copy(k_grouped[h][:].bitcast(word), words.rearrange("p u c -> p c u"))
+        def weave(c):
+            nc.scalar.copy(k_grouped[c][:].bitcast(U32), pair_words[:, quarters[c], :])
 
-        def quantize_keys(h):
+        def quantize_keys(c):
             nc.vector.quantize_mx(
-                out=k_codes[:, halves[h]].bitcast(FP8X4),
-                scales=k_scales[:, halves[h]],
-                in_=k_grouped[h][:].rearrange("p c t -> p (c t)"),
+                out=k_codes[:, quarters[c]].bitcast(FP8X4),
+                scales=k_scales[:, quarters[c]],
+                in_=k_grouped[c][:].rearrange("p c t -> p (c t)"),
             )
 
-        gather_plane(0)
-        gather_plane(1)
-        gather_scales(slice(0, N - P))
-        gather_plane(2)
-        gather_plane(3)
-        weave(0, nc.scalar.copy, U32)
-        weave(1, nc.scalar.copy, U32)
+        gather_plane(0, [whole])
+        gather_plane(1, [whole])
+        gather_plane(2, [whole])
+        gather_scales(quarters[2])
+        gather_plane(3, quarters)
+        for c in range(4):
+            weave(c)
         group_queries(0, nc.vector.tensor_copy)
         group_queries(1, nc.scalar.copy)
         quantize_keys(0)
         quantize_queries(0)
-        score(0, halves[0])
         quantize_keys(1)
-        score(0, halves[1])
+        score(0, halves[0], quarters[0:2])
+        quantize_keys(2)
+        quantize_keys(3)
+        score(0, halves[1], quarters[2:4])
+        gather_scales(halves[0])
         quantize_queries(1)
         group_queries(2, nc.vector.tensor_copy, pieces=2)
-        gather_scales(slice(N - P, N))
+        gather_scales(quarters[3])
         quantize_queries(2)
         place(0, whole)
         store(0)
         group_queries(3, nc.scalar.copy, "q_codes0")
         quantize_queries(3, "ts_pool")
         for m in (1, 2, 3):
-            score(m, whole)
+            for cols in halves if m == 1 else [whole]:
+                score(m, cols, [cols])
             place(m, whole)
             store(m)

@@ -83,7 +83,7 @@ def tile_attend_sddmm_ts_kernel(tc, qT, kT, ts, offs, out):
         ts_pool = sb([P, T], F32, "ts_pool")
         ts_by_col = ts_pool[:].rearrange("p (n j) -> p n j", n=P)
         for h in range(2):
-            bank = psum.tile([P, 4, P], F32, name="ts_bank%d" % h)
+            bank = psum.tile([P, 4, P], F32, name="ts_bank%d" % h, tag="ts_bank%d" % h)
             for j in range(4):
                 nc.tensor.transpose(bank[:, j, :], ts_cols[:, 4 * h + j : 4 * h + j + 1].to_broadcast([P, P]), ident[:])
             nc.scalar.copy(ts_by_col[:, :, 4 * h : 4 * h + 4], bank[:].rearrange("p j n -> p n j"))
@@ -112,7 +112,8 @@ def tile_attend_sddmm_ts_kernel(tc, qT, kT, ts, offs, out):
         def score(m, cols, passes):
             if m not in scores:
                 scores[m] = sb([P, N], F32, "scores%d" % m)
-            acc = psum.tile([P, cols.stop - cols.start], F32, name="acc%d_%d" % (m, cols.start))
+            name = "acc%d_%d" % (m, cols.start)
+            acc = psum.tile([P, cols.stop - cols.start], F32, name=name, tag="ts_bank0" if m == 3 else name)
             for part in passes:
                 nc.tensor.matmul_mx(
                     out=acc[:, part.start - cols.start : part.stop - cols.start],
@@ -167,9 +168,9 @@ def tile_attend_sddmm_ts_kernel(tc, qT, kT, ts, offs, out):
         quantize_queries(0)
         quantize_keys(1)
         score(0, halves[0], quarters[0:2])
-        quantize_keys(2)
-        quantize_keys(3)
-        score(0, halves[1], quarters[2:4])
+        for c in (2, 3):
+            quantize_keys(c)
+            score(0, quarters[c], [quarters[c]])
         gather_scales(halves[0])
         quantize_queries(1)
         group_queries(2, nc.vector.tensor_copy, pieces=2)

@@ -51,7 +51,7 @@ def tile_attend_sddmm_ts_kernel(tc, qT, kT, ts, offs, out):
 
         q_raw = []
         ts_at = 2 * N - half
-        raw_at = ts_at + N - P // 2
+        raw_at = ts_at + N
         shared = sb([P, raw_at + PACK * P], F32, "shared")
         ts_listed = shared[:, ts_at : ts_at + N]
         for m in range(NQ // P):
@@ -67,9 +67,9 @@ def tile_attend_sddmm_ts_kernel(tc, qT, kT, ts, offs, out):
         row_in_quad = sb([P, QUAD], F32, "row_in_quad")
         quad_start = sb([P, 1], F32, "quad_start")
         ident = sb([P, P], F32, "ident")
+        nc.gpsimd.memset(ones[:], 1.0)
         for g in range(P // QUAD):
             nc.gpsimd.memset(quad_start[g * QUAD : (g + 1) * QUAD, :], float(-g * QUAD))
-        nc.vector.memset(ones[:], 1.0)
         nc.vector.tensor_tensor_scan(col_no[:], ones[:], ones[:], 0.0, MULT, ADD)
         nc.vector.transpose(row_in_quad[:], col_no[:, 0:QUAD])
         nc.vector.tensor_scalar(ident[:], col_no[:], quad_start[:], row_in_quad[:, 0:1], ADD, IS_EQUAL)
@@ -77,7 +77,9 @@ def tile_attend_sddmm_ts_kernel(tc, qT, kT, ts, offs, out):
         windows = []
         for m in range(NQ // P):
             window = keep.tile([P, T], F32, name="window%d" % m)
-            nc.vector.memset(window[:], 0.0)
+            width = T // 4 if m == 0 else T
+            for c in range(0, T, width):
+                nc.vector.memset(window[:, c : c + width], 0.0)
             windows.append(window)
 
         ts_pool = sb([P, T], F32, "ts_pool")
@@ -113,7 +115,7 @@ def tile_attend_sddmm_ts_kernel(tc, qT, kT, ts, offs, out):
             if m not in scores:
                 scores[m] = sb([P, N], F32, "scores%d" % m)
             name = "acc%d_%d" % (m, cols.start)
-            acc = psum.tile([P, cols.stop - cols.start], F32, name=name, tag="ts_bank0" if m == 3 else name)
+            acc = psum.tile([P, cols.stop - cols.start], F32, name=name, tag="ts_bank%d" % (m - 2) if m >= 2 else name)
             for part in passes:
                 nc.tensor.matmul_mx(
                     out=acc[:, part.start - cols.start : part.stop - cols.start],
@@ -157,8 +159,8 @@ def tile_attend_sddmm_ts_kernel(tc, qT, kT, ts, offs, out):
 
         gather_plane(0, [whole])
         gather_plane(1, [whole])
+        gather_scales(halves[1])
         gather_plane(2, [whole])
-        gather_scales(quarters[2])
         gather_plane(3, quarters)
         for c in range(4):
             weave(c)
@@ -166,15 +168,13 @@ def tile_attend_sddmm_ts_kernel(tc, qT, kT, ts, offs, out):
         group_queries(1, nc.scalar.copy)
         quantize_keys(0)
         quantize_queries(0)
-        quantize_keys(1)
-        score(0, halves[0], quarters[0:2])
-        for c in (2, 3):
-            quantize_keys(c)
+        for c in range(4):
+            if c:
+                quantize_keys(c)
             score(0, quarters[c], [quarters[c]])
         gather_scales(halves[0])
+        group_queries(2, nc.vector.tensor_copy)
         quantize_queries(1)
-        group_queries(2, nc.vector.tensor_copy, pieces=2)
-        gather_scales(quarters[3])
         quantize_queries(2)
         place(0, whole)
         store(0)

@@ -50,7 +50,7 @@ def tile_attend_sddmm_ts_kernel(tc, qT, kT, ts, offs, out):
                 nc.sync.dma_start(offsets[:], offs)
 
         q_raw = []
-        ts_at = 2 * N - half
+        ts_at = 2 * N - P
         raw_at = ts_at + N
         shared = sb([P, raw_at + PACK * P], F32, "shared")
         ts_listed = shared[:, ts_at : ts_at + N]
@@ -161,6 +161,7 @@ def tile_attend_sddmm_ts_kernel(tc, qT, kT, ts, offs, out):
         gather_plane(1, [whole])
         gather_scales(halves[1])
         gather_plane(2, [whole])
+        gather_scales(quarters[1])
         gather_plane(3, quarters)
         for c in range(4):
             weave(c)
@@ -172,7 +173,7 @@ def tile_attend_sddmm_ts_kernel(tc, qT, kT, ts, offs, out):
             if c:
                 quantize_keys(c)
             score(0, quarters[c], [quarters[c]])
-        gather_scales(halves[0])
+        gather_scales(quarters[0])
         group_queries(2, nc.vector.tensor_copy)
         quantize_queries(1)
         quantize_queries(2)

@@ -174,10 +174,11 @@ def tile_attend_sddmm_ts_kernel(tc, qT, kT, ts, offs, out):
                 quantize_keys(c)
             score(0, quarters[c], [quarters[c]])
         gather_scales(quarters[0])
-        group_queries(2, nc.vector.tensor_copy)
         quantize_queries(1)
+        group_queries(2, nc.vector.tensor_copy, "q_raw1")
+        place(0, quarters[0])
         quantize_queries(2)
-        place(0, whole)
+        place(0, slice(P, N))
         store(0)
         group_queries(3, nc.scalar.copy, "q_codes0")
         quantize_queries(3, "ts_pool")

@@ -50,17 +50,14 @@ def tile_attend_sddmm_ts_kernel(tc, qT, kT, ts, offs, out):
                 nc.sync.dma_start(offsets[:], offs)
 
         q_raw = []
-        ts_at = 2 * N - P
-        raw_at = ts_at + N
-        shared = sb([P, raw_at + PACK * P], F32, "shared")
-        ts_listed = shared[:, ts_at : ts_at + N]
         for m in range(NQ // P):
-            if m == 2:
-                raw = shared[:, raw_at:].rearrange("p (t c) -> p t c", t=PACK)
-            else:
-                raw = sb([P, PACK, P], F32, "q_raw%d" % m)[:]
-            nc.sync.dma_start(raw, q_rows[:, :, m * P : (m + 1) * P])
+            raw = sb([P, PACK, P], F32, "q_raw%d" % m)
+            nc.sync.dma_start(raw[:], q_rows[:, :, m * P : (m + 1) * P])
             q_raw.append(raw)
+
+        ts_at = 2 * N - P
+        shared = sb([P, ts_at + N], F32, "shared")
+        ts_listed = shared[:, ts_at : ts_at + N]
 
         ones = sb([P, P], F32, "ones")
         col_no = sb([P, P], F32, "col_no")
@@ -85,7 +82,7 @@ def tile_attend_sddmm_ts_kernel(tc, qT, kT, ts, offs, out):
         ts_pool = sb([P, T], F32, "ts_pool")
         ts_by_col = ts_pool[:].rearrange("p (n j) -> p n j", n=P)
         for h in range(2):
-            bank = psum.tile([P, 4, P], F32, name="ts_bank%d" % h, tag="ts_bank%d" % h)
+            bank = psum.tile([P, 4, P], F32, name="ts_bank%d" % h, tag="bank%d" % h)
             for j in range(4):
                 nc.tensor.transpose(bank[:, j, :], ts_cols[:, 4 * h + j : 4 * h + j + 1].to_broadcast([P, P]), ident[:])
             nc.scalar.copy(ts_by_col[:, :, 4 * h : 4 * h + 4], bank[:].rearrange("p j n -> p n j"))
@@ -95,41 +92,42 @@ def tile_attend_sddmm_ts_kernel(tc, qT, kT, ts, offs, out):
 
         q_codes, q_scales, q_grouped, scores = {}, {}, {}, {}
 
-        def group_queries(m, copy, tag=None, pieces=1):
-            grouped = sb([P, P, PACK], BF16, "q_grouped%d" % m, tag)
-            for c in range(0, P, P // pieces):
-                cols = slice(c, c + P // pieces)
-                copy(
-                    grouped[:, cols, :].rearrange("p (c i) t -> p c t i", i=4),
-                    q_raw[m][:, :, cols].rearrange("p t (c i) -> p c t i", i=4),
-                )
-            q_grouped[m] = grouped
+        def group_queries(m, copy, cols=slice(0, P), tag=None):
+            grouped = sb([P, cols.stop - cols.start, PACK], BF16, "q_grouped%d_%d" % (m, cols.start), tag)
+            copy(
+                grouped[:].rearrange("p (c i) t -> p c t i", i=4),
+                q_raw[m][:, :, cols].rearrange("p t (c i) -> p c t i", i=4),
+            )
+            q_grouped.setdefault(m, []).append((cols, grouped))
 
         def quantize_queries(m, tag=None):
-            codes = sb([P, P], U32, "q_codes%d" % m, tag)
-            scales = sb([P, P], U8, "q_scales%d" % m)
-            nc.vector.quantize_mx(out=codes[:].bitcast(FP8X4), scales=scales[:], in_=q_grouped[m][:].rearrange("p c t -> p (c t)"))
-            q_codes[m], q_scales[m] = codes, scales
-
-        def score(m, cols, passes):
-            if m not in scores:
-                scores[m] = sb([P, N], F32, "scores%d" % m)
-            name = "acc%d_%d" % (m, cols.start)
-            acc = psum.tile([P, cols.stop - cols.start], F32, name=name, tag="ts_bank%d" % (m - 2) if m >= 2 else name)
-            for part in passes:
-                nc.tensor.matmul_mx(
-                    out=acc[:, part.start - cols.start : part.stop - cols.start],
-                    lhsT=q_codes[m][:].bitcast(FP8X4),
-                    lhsT_scale=q_scales[m][:],
-                    rhs=k_codes[:, part].bitcast(FP8X4),
-                    rhs_scale=k_scales[:, part],
-                    start=True,
-                    stop=True,
+            q_codes[m] = sb([P, P], U32, "q_codes%d" % m, tag)
+            q_scales[m] = sb([P, P], U8, "q_scales%d" % m)
+            for cols, grouped in q_grouped[m]:
+                nc.vector.quantize_mx(
+                    out=q_codes[m][:, cols].bitcast(FP8X4),
+                    scales=q_scales[m][:, cols],
+                    in_=grouped[:].rearrange("p c t -> p (c t)"),
                 )
-            nc.scalar.copy(scores[m][:, cols], acc[:])
 
-        def place(m, cols):
-            nc.vector.tensor_tensor(listed(windows[m], cols), scores[m][:, cols], ts_listed[:, cols], MULT)
+        def scores_tile(m, run, tag=None):
+            scores[m, run.start] = sb([P, run.stop - run.start], F32, "scores%d_%d" % (m, run.start), tag)
+
+        def score(m, run, cols, bank):
+            acc = psum.tile([P, cols.stop - cols.start], F32, name="acc%d_%d" % (m, cols.start), tag="bank%d" % bank)
+            nc.tensor.matmul_mx(
+                out=acc[:],
+                lhsT=q_codes[m][:].bitcast(FP8X4),
+                lhsT_scale=q_scales[m][:],
+                rhs=k_codes[:, cols].bitcast(FP8X4),
+                rhs_scale=k_scales[:, cols],
+                start=True,
+                stop=True,
+            )
+            nc.scalar.copy(scores[m, run.start][:, cols.start - run.start : cols.stop - run.start], acc[:])
+
+        def place(m, run):
+            nc.vector.tensor_tensor(listed(windows[m], run), scores[m, run.start][:], ts_listed[:, run], MULT)
 
         def store(m):
             nc.sync.dma_start(out_rows[:, m, :], windows[m][:])
@@ -169,21 +167,25 @@ def tile_attend_sddmm_ts_kernel(tc, qT, kT, ts, offs, out):
         group_queries(1, nc.scalar.copy)
         quantize_keys(0)
         quantize_queries(0)
-        for c in range(4):
-            if c:
-                quantize_keys(c)
-            score(0, quarters[c], [quarters[c]])
-        gather_scales(quarters[0])
+        first, rest = quarters[0], slice(P, N)
+        scores_tile(0, first)
+        scores_tile(0, rest)
+        score(0, first, first, 2)
+        for c in (1, 2, 3):
+            quantize_keys(c)
+            score(0, rest, quarters[c], 2 + c)
+        gather_scales(first)
         quantize_queries(1)
-        group_queries(2, nc.vector.tensor_copy, "q_raw1")
-        place(0, quarters[0])
+        group_queries(2, nc.vector.tensor_copy, tag="q_raw1")
+        place(0, first)
         quantize_queries(2)
-        place(0, slice(P, N))
+        place(0, rest)
         store(0)
-        group_queries(3, nc.scalar.copy, "q_codes0")
+        group_queries(3, nc.scalar.copy, tag="q_codes0")
         quantize_queries(3, "ts_pool")
-        for m in (1, 2, 3):
-            for cols in halves if m == 1 else [whole]:
-                score(m, cols, [cols])
+        for m, banks in ((1, (6, 7)), (2, (0, 1)), (3, (2, 3))):
+            scores_tile(m, whole)
+            for cols, bank in zip(halves, banks):
+                score(m, whole, cols, bank)
             place(m, whole)
             store(m)

@@ -175,8 +175,8 @@ def tile_attend_sddmm_ts_kernel(tc, qT, kT, ts, offs, out):
             quantize_keys(c)
             score(0, rest, quarters[c], 2 + c)
         gather_scales(first)
+        group_queries(2, nc.vector.tensor_copy)
         quantize_queries(1)
-        group_queries(2, nc.vector.tensor_copy, tag="q_raw1")
         place(0, first)
         quantize_queries(2)
         place(0, rest)

from contextlib import ExitStack

import concourse.mybir as mybir

D_FEAT, NQ, T, N = 512, 512, 1024, 512
P = 128
PACK = 4
QUAD = 32
FLOPS = 2 * D_FEAT * NQ * N

F32 = mybir.dt.float32
BF16 = mybir.dt.bfloat16
I32 = mybir.dt.int32
U32 = mybir.dt.uint32
U16 = mybir.dt.uint16
U8 = mybir.dt.uint8
FP8X4 = mybir.dt.float8_e4m3fn_x4
MULT = mybir.AluOpType.mult
ADD = mybir.AluOpType.add
IS_EQUAL = mybir.AluOpType.is_equal


def tile_attend_sddmm_ts_kernel(tc, qT, kT, ts, offs, out):
    nc = tc.nc
    k_rows = kT.rearrange("(p t) w -> p t w", t=PACK)
    q_rows = qT.rearrange("b (p t) q -> p (b t) q", t=PACK)
    out_rows = out.rearrange("b (m p) w -> p (b m) w", p=P)
    half = N // 2
    whole, halves = slice(0, N), (slice(0, half), slice(half, N))
    quarters = [slice(c, c + P) for c in range(0, N, P)]

    with ExitStack() as ctx:
        keep = ctx.enter_context(tc.tile_pool(name="keep", bufs=1))
        psum = ctx.enter_context(tc.psum_pool(name="psum", bufs=1))

        def sb(shape, dtype, name, tag=None):
            return keep.tile(shape, dtype, name=name, tag=tag or name, align_bytes=64)

        offsets = keep.tile([P, N // 16], U16, name="offsets")

        ts_cols = sb([P, T // P], F32, "ts_cols")
        nc.scalar.dma_start(ts_cols[:], ts[0:1, :].rearrange("o (p j) -> (o p) j", p=P))

        k_pool = []
        for t in range(PACK):
            plane = sb([P, T], F32, "k_plane%d" % t)
            nc.sync.dma_start(plane[:], k_rows[:, t, :])
            k_pool.append(plane)
            if t == 0:
                nc.sync.dma_start(offsets[:], offs)

        q_raw = []
        for m in range(NQ // P):
            raw = sb([P, PACK, P], F32, "q_raw%d" % m)
            nc.sync.dma_start(raw[:], q_rows[:, :, m * P : (m + 1) * P])
            q_raw.append(raw)

        ts_at = 2 * N - P
        shared = sb([P, ts_at + N], F32, "shared")
        ts_listed = shared[:, ts_at : ts_at + N]

        ones = sb([P, P], F32, "ones")
        col_no = sb([P, P], F32, "col_no")
        row_in_quad = sb([P, QUAD], F32, "row_in_quad")
        quad_start = sb([P, 1], F32, "quad_start")
        ident = sb([P, P], F32, "ident")
        nc.gpsimd.memset(ones[:], 1.0)
        for g in range(P // QUAD):
            nc.gpsimd.memset(quad_start[g * QUAD : (g + 1) * QUAD, :], float(-g * QUAD))
        nc.vector.tensor_tensor_scan(col_no[:], ones[:], ones[:], 0.0, MULT, ADD)
        nc.vector.transpose(row_in_quad[:], col_no[:, 0:QUAD])
        nc.vector.tensor_scalar(ident[:], col_no[:], quad_start[:], row_in_quad[:, 0:1], ADD, IS_EQUAL)

        windows = []
        for m in range(NQ // P):
            window = keep.tile([P, T], F32, name="window%d" % m)
            width = T // 4 if m == 0 else T
            for c in range(0, T, width):
                nc.vector.memset(window[:, c : c + width], 0.0)
            windows.append(window)

        ts_pool = sb([P, T], F32, "ts_pool")
        ts_by_col = ts_pool[:].rearrange("p (n j) -> p n j", n=P)
        for h in range(2):
            bank = psum.tile([P, 4, P], F32, name="ts_bank%d" % h, tag="bank%d" % h)
            for j in range(4):
                nc.tensor.transpose(bank[:, j, :], ts_cols[:, 4 * h + j : 4 * h + j + 1].to_broadcast([P, P]), ident[:])
            nc.scalar.copy(ts_by_col[:, :, 4 * h : 4 * h + 4], bank[:].rearrange("p j n -> p n j"))

        def listed(tile, cols):
            return tile[:].indirect(offsets[:, cols.start // 16 : cols.stop // 16])

        q_codes, q_scales, q_grouped, scores = {}, {}, {}, {}

        def group_queries(m, copy, cols=slice(0, P), tag=None):
            grouped = sb([P, cols.stop - cols.start, PACK], BF16, "q_grouped%d_%d" % (m, cols.start), tag)
            copy(
                grouped[:].rearrange("p (c i) t -> p c t i", i=4),
                q_raw[m][:, :, cols].rearrange("p t (c i) -> p c t i", i=4),
            )
            q_grouped.setdefault(m, []).append((cols, grouped))

        def quantize_queries(m, tag=None):
            q_codes[m] = sb([P, P], U32, "q_codes%d" % m, tag)
            q_scales[m] = sb([P, P], U8, "q_scales%d" % m)
            for cols, grouped in q_grouped[m]:
                nc.vector.quantize_mx(
                    out=q_codes[m][:, cols].bitcast(FP8X4),
                    scales=q_scales[m][:, cols],
                    in_=grouped[:].rearrange("p c t -> p (c t)"),
                )

        def scores_tile(m, run, tag=None):
            scores[m, run.start] = sb([P, run.stop - run.start], F32, "scores%d_%d" % (m, run.start), tag)

        def score(m, run, cols, bank):
            acc = psum.tile([P, cols.stop - cols.start], F32, name="acc%d_%d" % (m, cols.start), tag="bank%d" % bank)
            nc.tensor.matmul_mx(
                out=acc[:],
                lhsT=q_codes[m][:].bitcast(FP8X4),
                lhsT_scale=q_scales[m][:],
                rhs=k_codes[:, cols].bitcast(FP8X4),
                rhs_scale=k_scales[:, cols],
                start=True,
                stop=True,
            )
            nc.scalar.copy(scores[m, run.start][:, cols.start - run.start : cols.stop - run.start], acc[:])

        def place(m, run):
            nc.vector.tensor_tensor(listed(windows[m], run), scores[m, run.start][:], ts_listed[:, run], MULT)

        def store(m):
            nc.sync.dma_start(out_rows[:, m, :], windows[m][:])

        pairs = shared[:, 0 : 2 * N].bitcast(BF16).rearrange("p (u c e) -> p u c e", u=2, e=2)
        pair_words = shared[:, 0 : 2 * N].bitcast(U32).rearrange("p (u c) -> p c u", u=2)
        k_grouped = [sb([P, P, PACK], BF16, "k_grouped%d" % c) for c in range(4)]
        k_codes = sb([P, N], U32, "k_codes")
        k_scales = sb([P, N], U8, "k_scales")

        def gather_plane(t, pieces):
            for cols in pieces:
                nc.vector.tensor_copy(pairs[:, t // 2, cols, t % 2], listed(k_pool[t], cols))

        def gather_scales(cols):
            nc.vector.tensor_copy(ts_listed[:, cols], listed(ts_pool, cols))

        def weave(c):
            nc.scalar.copy(k_grouped[c][:].bitcast(U32), pair_words[:, quarters[c], :])

        def quantize_keys(c):
            nc.vector.quantize_mx(
                out=k_codes[:, quarters[c]].bitcast(FP8X4),
                scales=k_scales[:, quarters[c]],
                in_=k_grouped[c][:].rearrange("p c t -> p (c t)"),
            )

        gather_plane(0, [whole])
        gather_plane(1, [whole])
        gather_scales(halves[1])
        gather_plane(2, [whole])
        gather_scales(quarters[1])
        gather_plane(3, quarters)
        for c in range(4):
            weave(c)
        group_queries(0, nc.vector.tensor_copy)
        group_queries(1, nc.scalar.copy)
        quantize_keys(0)
        quantize_queries(0)
        first, rest = quarters[0], slice(P, N)
        scores_tile(0, first)
        scores_tile(0, rest)
        score(0, first, first, 2)
        for c in (1, 2, 3):
            quantize_keys(c)
            score(0, rest, quarters[c], 2 + c)
        gather_scales(first)
        group_queries(2, nc.vector.tensor_copy)
        quantize_queries(1)
        place(0, first)
        quantize_queries(2)
        place(0, rest)
        store(0)
        group_queries(3, nc.scalar.copy, tag="q_codes0")
        quantize_queries(3, "ts_pool")
        for m, banks in ((1, (6, 7)), (2, (0, 1)), (3, (2, 3))):
            scores_tile(m, whole)
            for cols, bank in zip(halves, banks):
                score(m, whole, cols, bank)
            place(m, whole)
            store(m)
